import numpy as np
import ml_dtypes


def mxq(x, axis, fmt="e4m3"):
    dtype, down = {"e4m3": (ml_dtypes.float8_e4m3fn, 7), "e5m2": (ml_dtypes.float8_e5m2, 14)}[fmt]
    v = np.moveaxis(np.asarray(x, np.float32).astype(ml_dtypes.bfloat16).astype(np.float64), axis, -1)
    blocks = v.reshape(v.shape[:-1] + (-1, 32))
    amax = np.abs(blocks).max(-1, keepdims=True)
    byte = np.maximum(np.where(amax > 0, np.frexp(amax)[1] - 1 + 127, 0) - down, 1)
    scale = np.exp2(byte - 127.0)
    codes = (blocks / scale).astype(np.float32).astype(dtype).astype(np.float64)
    return np.moveaxis((codes * scale).reshape(v.shape), -1, axis)


WIDE = False


def mx_kscale(k):
    if not WIDE:
        return np.ones(k)
    levels = np.array([10, -10, 5, -5, 0])
    if k % 512:
        return np.exp2(np.random.permutation(np.resize(levels, k // 32))).repeat(32)
    a = np.empty((k // 512, 16))
    for p in range(k // 512):
        a[p, :8] = np.random.permutation(np.resize(levels, 8))
        for g in range(8):
            far = levels[np.abs(levels - a[p, g]) >= 10]
            a[p, g + 8] = far[np.random.randint(len(far))]
    return np.exp2(a.ravel()).repeat(32)


def f64(x):
    return np.asarray(x).astype(np.float64)


def striped(idx):
    return np.tile(idx.reshape(-1, 16).T, (8, 1)).astype(np.uint16)


def unstriped(offs):
    return offs[:16].T.reshape(-1).astype(np.int64)


def pack_weight(w):
    k, n = w.shape
    w = f64(np.asarray(w, np.float32).astype(ml_dtypes.bfloat16)).reshape(k // 32, 32, n)
    amax = np.abs(w).max(1)
    byte = np.clip(np.where(amax > 0, np.frexp(amax)[1] - 1 + 127 - 7, 1), 1, 254)
    scaled = (w * np.exp2(127.0 - byte)[:, None, :]).reshape(k, n).astype(np.float32)
    words = np.ascontiguousarray(scaled.reshape(k // 512, 128, 4, n).transpose(0, 1, 3, 2)).astype(ml_dtypes.float8_e4m3fn).view(np.uint8)
    return words, np.ascontiguousarray(byte.astype(np.uint8).reshape(k // 512, 16, n))


def unpack_weight(words, scales):
    g, p, n, _ = words.shape
    vals = np.ascontiguousarray(words).view(ml_dtypes.float8_e4m3fn).astype(np.float64) * np.repeat(np.exp2(scales.astype(np.float64) - 127.0), 8, axis=1)[..., None]
    return vals.transpose(0, 1, 3, 2).reshape(g * 512, n)


def sigmoid(v):
    return 1.0 / (1.0 + np.exp(-np.maximum(v, -700.0)))


K, T, S, D, N = 512, 2048, 1024, 4, 256
P = 2 ** 7


def setup_inputs():
    n = np.random.standard_normal
    s = mx_kscale(K)[:, None]
    packed_xT = pack_weight(n((K, T)) * s)
    return {
        "x_words": packed_xT[0],
        "x_scales": packed_xT[1],
        "w1": (n((K, N)) / np.sqrt(K) / s).astype(np.float32),
        "prior": (np.tile(n(S) * 0.7, (P, 1))).astype(np.float32),
        "wgt": (np.tile(np.random.uniform(0.3, 0.95, S), (P, 1))).astype(np.float32),
        "offs": striped(np.random.permutation(T)[:S]),
    }


def reference(x_words, x_scales, w1, prior, wgt, offs):
    xq = unpack_weight(x_words, x_scales)[:, unstriped(offs)]
    y = mxq(f64(w1), 0, "e4m3").T @ xq
    t1 = y - 0.8
    t0 = 1.2 * (y + 0.3)
    post = sigmoid(-0.7 * ((t1) ** 2) - (-1.0 * (t0 + np.exp(-1.0 * t0))) + f64(prior)[:1])
    lg = np.log(-1.0 * (post * f64(wgt)[:1]) + 1.0)
    return -1.0 * (np.exp(lg.reshape(len(lg), -1, D).sum(axis=2))) + 1.0

@@ -1,0 +1,131 @@
+import math
+from contextlib import ExitStack
+
+import concourse.mybir as mybir
+from concourse.masks import make_identity
+
+K, T, S, D, N = 512, 2048, 1024, 4, 256
+P = 128
+HALVES = S // (D * P)
+FLOPS = 2 * K * S * N
+BYTES = K * T + (K // 32) * T + K * N * 4 + 2 * S * 4 + P * (S // 16) * 2 + N * (S // D) * 4
+
+F32 = mybir.dt.float32
+BF16 = mybir.dt.bfloat16
+I32 = mybir.dt.int32
+U32 = mybir.dt.uint32
+U16 = mybir.dt.uint16
+U8 = mybir.dt.uint8
+FP8X4 = mybir.dt.float8_e4m3fn_x4
+ALU = mybir.AluOpType
+ACT = mybir.ActivationFunctionType
+
+CENTRE = (2 * 0.7 * 0.8 + 1.2) / (2 * 0.7)
+OFFSET = 0.7 * CENTRE * CENTRE - 0.7 * 0.8 * 0.8 + 1.2 * 0.3
+ROOT = math.sqrt(0.7 / 2)
+TINY = 1e-9
+
+
+def tile_picked_yprot_prob_p_kernel(tc, x_words, x_scales, w1, prior, wgt, offs, out):
+    nc = tc.nc
+    with ExitStack() as ctx:
+        keep = ctx.enter_context(tc.tile_pool(name="keep", bufs=1))
+        psum = ctx.enter_context(tc.psum_pool(name="psum", bufs=1))
+
+        offsets = keep.tile([P, S // 16], U16, name="offsets")
+        nc.sync.dma_start(offsets[:], offs)
+
+        scale_table = keep.tile([P, T], U8, name="scale_table", align_bytes=64)
+        for q in range(4):
+            nc.sync.dma_start(scale_table[32 * q : 32 * q + 32, :].bitcast(I32), x_scales[0, 4 * q : 4 * q + 4, :].bitcast(I32).partition_broadcast(8))
+
+        weight = keep.tile([P, HALVES, D], F32, name="weight")
+        nc.scalar.dma_start(weight[:], wgt[0].rearrange("(h p d) -> p h d", h=HALVES, d=D))
+        w_raw = keep.tile([P, 4, N], F32, name="w_raw")
+        nc.sync.dma_start(w_raw[:], w1.rearrange("(p j) m -> p j m", j=4))
+        word_table = keep.tile([P, T], I32, name="word_table", align_bytes=64)
+        nc.sync.dma_start(word_table[:], x_words[0].rearrange("p c r -> p (c r)").bitcast(I32))
+        log_odds = keep.tile([P, HALVES, D], F32, name="log_odds")
+        nc.scalar.dma_start(log_odds[:], prior[0].rearrange("(h p d) -> p h d", h=HALVES, d=D))
+
+        identity = keep.tile([P, P], F32, name="identity")
+        make_identity(nc, identity[:])
+
+        warm = keep.tile([P, 1], F32, name="warm")
+        nc.scalar.activation(warm[:], identity[:, 0:1], ACT.Exp)
+
+        scale_dealt = []
+        for h in range(HALVES):
+            picked = keep.tile([P, D * P], U8, name="picked_scales%d" % h, align_bytes=64)
+            nc.vector.tensor_copy(picked[:], scale_table[:].indirect(offsets[:, 32 * h : 32 * h + 32]))
+            dealt = keep.tile([P, D, P], U8, name="dealt_scales%d" % h, align_bytes=64)
+            nc.vector.tensor_copy(dealt[:], picked[:].rearrange("p (v d) -> p d v", d=D))
+            scale_dealt.append(dealt)
+
+        w_grouped = keep.tile([P, N, 4], BF16, name="w_grouped", align_bytes=64)
+        nc.scalar.copy(w_grouped[:].rearrange("p (c i) j -> p c j i", i=4), w_raw[:].rearrange("p j (c i) -> p c j i", i=4))
+        w_codes = keep.tile([P, N], U32, name="w_codes", align_bytes=64)
+        w_scales = keep.tile([P, N], U8, name="w_scales", align_bytes=64)
+        nc.vector.quantize_mx(out=w_codes[:].bitcast(FP8X4), scales=w_scales[:], in_=w_grouped[:].rearrange("p m j -> p (m j)"))
+
+        squared = keep.tile([P, HALVES, D], F32, name="squared")
+        nc.gpsimd.tensor_tensor(squared[:], weight[:], weight[:], ALU.mult)
+        nudge = keep.tile([P, HALVES, D], F32, name="nudge")
+        nc.gpsimd.tensor_scalar(nudge[:], squared[:], TINY * TINY, 2 * TINY, ALU.is_lt, ALU.mult)
+        safe = keep.tile([P, HALVES, D], F32, name="safe")
+        nc.gpsimd.tensor_tensor(safe[:], weight[:], nudge[:], ALU.add)
+        inverse = keep.tile([P, HALVES, D], F32, name="inverse")
+        nc.vector.reciprocal(inverse[:], safe[:])
+        root = keep.tile([P, HALVES, D], F32, name="root")
+        nc.gpsimd.tensor_scalar(root[:], inverse[:], 2.0, -1.0, ALU.mult, ALU.add)
+        slope = keep.tile([P, HALVES, D], F32, name="slope")
+        nc.gpsimd.tensor_scalar(slope[:], safe[:], -0.5, 0.0, ALU.mult, ALU.add)
+        pair = keep.tile([P, HALVES], F32, name="pair")
+        nc.gpsimd.tensor_tensor(pair[:], slope[:, :, 1], slope[:, :, 2], ALU.mult)
+        later = keep.tile([P, HALVES], F32, name="later")
+        nc.gpsimd.tensor_tensor(later[:], pair[:], slope[:, :, 3], ALU.mult)
+        first_slope = keep.tile([P, HALVES], F32, name="first_slope")
+        nc.gpsimd.tensor_tensor(first_slope[:], later[:], slope[:, :, 0], ALU.mult)
+        first_level = keep.tile([P, HALVES], F32, name="first_level")
+        nc.gpsimd.tensor_tensor(first_level[:], first_slope[:], later[:], ALU.add)
+        shift = keep.tile([P, HALVES, D], F32, name="shift")
+        nc.gpsimd.tensor_scalar(shift[:], log_odds[:], 0.5, 0.5 * OFFSET, ALU.mult, ALU.add)
+
+        for h in range(HALVES):
+            codes = keep.tile([P, D, P], U32, name="picked_words%d" % h, align_bytes=64)
+            nc.vector.tensor_copy(codes[:].rearrange("p d v -> p v d"), word_table[:].bitcast(U32).indirect(offsets[:, 32 * h : 32 * h + 32]))
+            running = None
+            for pr in range(D // 2):
+                bank = psum.tile([P, 2, N], F32, name="y%d%d" % (h, pr))
+                for e in range(2):
+                    d = 2 * pr + e
+                    nc.tensor.matmul_mx(out=bank[:, e, :], lhsT=codes[:, d, :].bitcast(FP8X4), lhsT_scale=scale_dealt[h][:, d, :],
+                                        rhs=w_codes[:].bitcast(FP8X4), rhs_scale=w_scales[:], start=True, stop=True)
+                tail = keep.tile([P, 2, N], F32, name="tail%d%d" % (h, pr))
+                nc.scalar.activation(tail[:], bank[:], ACT.Exp, bias=-1.2 * 0.3 + math.log(0.5), scale=-1.2)
+                bowl = keep.tile([P, 2, N], F32, name="bowl%d%d" % (h, pr))
+                nc.scalar.activation(bowl[:], bank[:], ACT.Square, bias=-ROOT * CENTRE, scale=ROOT)
+                half_logit = keep.tile([P, 2, N], F32, name="half_logit%d%d" % (h, pr))
+                for e in range(2):
+                    d = 2 * pr + e
+                    nc.vector.scalar_tensor_tensor(half_logit[:, e, :], tail[:, e, :], shift[:, h, d : d + 1], bowl[:, e, :], ALU.add, ALU.subtract)
+                th = keep.tile([P, 2, N], F32, name="th%d%d" % (h, pr))
+                if h == HALVES - 1 and pr == D // 2 - 1:
+                    for e in range(2):
+                        nc.scalar.activation(th[:, e, :], half_logit[:, e, :], ACT.Tanh)
+                else:
+                    nc.scalar.activation(th[:], half_logit[:], ACT.Tanh)
+                for e in range(2):
+                    d = 2 * pr + e
+                    nxt = keep.tile([P, N], F32, name="running%d%d" % (h, d))
+                    if d == 0:
+                        nc.vector.tensor_scalar(nxt[:], th[:, e, :], first_slope[:, h : h + 1], first_level[:, h : h + 1], ALU.mult, ALU.add)
+                    else:
+                        nc.vector.scalar_tensor_tensor(nxt[:], th[:, e, :], root[:, h, d : d + 1], running[:], ALU.subtract, ALU.mult)
+                    running = nxt
+            turned = psum.tile([P, N // P, P], F32, name="turned%d" % h)
+            for b in range(N // P):
+                nc.tensor.transpose(turned[:, b, :], running[:, b * P : (b + 1) * P], identity[:])
+            result = keep.tile([P, N // P, P], F32, name="result%d" % h)
+            nc.vector.tensor_scalar(result[:], turned[:], -1.0, 1.0, ALU.mult, ALU.add)
+            nc.sync.dma_start(out[:, h * P : (h + 1) * P].rearrange("(b p) v -> p b v", p=P), result[:])

@@ -24,6 +24,7 @@ CENTRE = (2 * 0.7 * 0.8 + 1.2) / (2 * 0.7)
 OFFSET = 0.7 * CENTRE * CENTRE - 0.7 * 0.8 * 0.8 + 1.2 * 0.3
 ROOT = math.sqrt(0.7 / 2)
 TINY = 1e-9
+LAG = 2
 
 
 def tile_picked_yprot_prob_p_kernel(tc, x_words, x_scales, w1, prior, wgt, offs, out):
@@ -35,24 +36,27 @@ def tile_picked_yprot_prob_p_kernel(tc, x_words, x_scales, w1, prior, wgt, offs,
         offsets = keep.tile([P, S // 16], U16, name="offsets")
         nc.sync.dma_start(offsets[:], offs)
 
+        weight = keep.tile([P, HALVES, D], F32, name="weight")
+        nc.gpsimd.dma_start(weight[:], wgt[0].rearrange("(h p d) -> p h d", h=HALVES, d=D))
+        log_odds = keep.tile([P, HALVES, D], F32, name="log_odds")
+        nc.gpsimd.dma_start(log_odds[:], prior[0].rearrange("(h p d) -> p h d", h=HALVES, d=D))
+
         scale_table = keep.tile([P, T], U8, name="scale_table", align_bytes=64)
         for q in range(4):
             nc.sync.dma_start(scale_table[32 * q : 32 * q + 32, :].bitcast(I32), x_scales[0, 4 * q : 4 * q + 4, :].bitcast(I32).partition_broadcast(8))
 
-        weight = keep.tile([P, HALVES, D], F32, name="weight")
-        nc.scalar.dma_start(weight[:], wgt[0].rearrange("(h p d) -> p h d", h=HALVES, d=D))
         w_raw = keep.tile([P, 4, N], F32, name="w_raw")
         nc.sync.dma_start(w_raw[:], w1.rearrange("(p j) m -> p j m", j=4))
         word_table = keep.tile([P, T], I32, name="word_table", align_bytes=64)
         nc.sync.dma_start(word_table[:], x_words[0].rearrange("p c r -> p (c r)").bitcast(I32))
-        log_odds = keep.tile([P, HALVES, D], F32, name="log_odds")
-        nc.scalar.dma_start(log_odds[:], prior[0].rearrange("(h p d) -> p h d", h=HALVES, d=D))
 
         identity = keep.tile([P, P], F32, name="identity")
         make_identity(nc, identity[:])
 
         warm = keep.tile([P, 1], F32, name="warm")
-        nc.scalar.activation(warm[:], identity[:, 0:1], ACT.Exp)
+        zero = keep.tile([P, 1], F32, name="zero")
+        nc.vector.memset(zero[:], 0.0)
+        nc.scalar.activation(warm[:], zero[:], ACT.Exp)
 
         scale_dealt = []
         for h in range(HALVES):
@@ -62,7 +66,7 @@ def tile_picked_yprot_prob_p_kernel(tc, x_words, x_scales, w1, prior, wgt, offs,
             nc.vector.tensor_copy(dealt[:], picked[:].rearrange("p (v d) -> p d v", d=D))
             scale_dealt.append(dealt)
 
-        w_grouped = keep.tile([P, N, 4], BF16, name="w_grouped", align_bytes=64)
+        w_grouped = keep.tile([P, N, 4], BF16, name="w_grouped", tag="words0", align_bytes=64)
         nc.scalar.copy(w_grouped[:].rearrange("p (c i) j -> p c j i", i=4), w_raw[:].rearrange("p j (c i) -> p c j i", i=4))
         w_codes = keep.tile([P, N], U32, name="w_codes", align_bytes=64)
         w_scales = keep.tile([P, N], U8, name="w_scales", align_bytes=64)
@@ -89,43 +93,74 @@ def tile_picked_yprot_prob_p_kernel(tc, x_words, x_scales, w1, prior, wgt, offs,
         first_level = keep.tile([P, HALVES], F32, name="first_level")
         nc.gpsimd.tensor_tensor(first_level[:], first_slope[:], later[:], ALU.add)
         shift = keep.tile([P, HALVES, D], F32, name="shift")
-        nc.gpsimd.tensor_scalar(shift[:], log_odds[:], 0.5, 0.5 * OFFSET, ALU.mult, ALU.add)
+        nc.scalar.activation(shift[:], log_odds[:], ACT.Copy, bias=0.5 * OFFSET, scale=0.5)
 
+        codes = []
         for h in range(HALVES):
-            codes = keep.tile([P, D, P], U32, name="picked_words%d" % h, align_bytes=64)
-            nc.vector.tensor_copy(codes[:].rearrange("p d v -> p v d"), word_table[:].bitcast(U32).indirect(offsets[:, 32 * h : 32 * h + 32]))
-            running = None
-            for pr in range(D // 2):
-                bank = psum.tile([P, 2, N], F32, name="y%d%d" % (h, pr))
-                for e in range(2):
-                    d = 2 * pr + e
-                    nc.tensor.matmul_mx(out=bank[:, e, :], lhsT=codes[:, d, :].bitcast(FP8X4), lhsT_scale=scale_dealt[h][:, d, :],
-                                        rhs=w_codes[:].bitcast(FP8X4), rhs_scale=w_scales[:], start=True, stop=True)
-                tail = keep.tile([P, 2, N], F32, name="tail%d%d" % (h, pr))
-                nc.scalar.activation(tail[:], bank[:], ACT.Exp, bias=-1.2 * 0.3 + math.log(0.5), scale=-1.2)
-                bowl = keep.tile([P, 2, N], F32, name="bowl%d%d" % (h, pr))
-                nc.scalar.activation(bowl[:], bank[:], ACT.Square, bias=-ROOT * CENTRE, scale=ROOT)
-                half_logit = keep.tile([P, 2, N], F32, name="half_logit%d%d" % (h, pr))
-                for e in range(2):
-                    d = 2 * pr + e
-                    nc.vector.scalar_tensor_tensor(half_logit[:, e, :], tail[:, e, :], shift[:, h, d : d + 1], bowl[:, e, :], ALU.add, ALU.subtract)
-                th = keep.tile([P, 2, N], F32, name="th%d%d" % (h, pr))
-                if h == HALVES - 1 and pr == D // 2 - 1:
-                    for e in range(2):
-                        nc.scalar.activation(th[:, e, :], half_logit[:, e, :], ACT.Tanh)
+            dealt_words = keep.tile([P, D, P], U32, name="picked_words%d" % h, tag="words%d" % h, align_bytes=64)
+            nc.vector.tensor_copy(dealt_words[:].rearrange("p d v -> p v d"), word_table[:].bitcast(U32).indirect(offsets[:, 32 * h : 32 * h + 32]))
+            codes.append(dealt_words)
+
+        tails = [keep.tile([P, D, N], F32, name="tail%d" % h) for h in range(HALVES)]
+        bowls = [keep.tile([P, D, N], F32, name="bowl%d" % h) for h in range(HALVES)]
+        half_logits = [keep.tile([P, D, N], F32, name="half_logit%d" % h) for h in range(HALVES)]
+        tanhs = [keep.tile([P, D, N], F32, name="tanh%d" % h) for h in range(HALVES)]
+        running = {}
+
+        def front(h, d0, d1, square_on_vector=False):
+            bank = psum.tile([P, d1 - d0, N], F32, name="y%d%d" % (h, d0), tag="y%d%d" % (h, d0))
+            for d in range(d0, d1):
+                nc.tensor.matmul_mx(out=bank[:, d - d0, :], lhsT=codes[h][:, d, :].bitcast(FP8X4), lhsT_scale=scale_dealt[h][:, d, :],
+                                    rhs=w_codes[:].bitcast(FP8X4), rhs_scale=w_scales[:], start=True, stop=True)
+            if square_on_vector:
+                centred = keep.tile([P, d1 - d0, N], F32, name="centred%d%d" % (h, d0))
+                nc.vector.tensor_scalar(centred[:], bank[:], -CENTRE, ROOT, ALU.add, ALU.mult)
+                nc.vector.tensor_tensor(bowls[h][:, d0:d1, :], centred[:], centred[:], ALU.mult)
+            nc.scalar.activation(tails[h][:, d0:d1, :], bank[:], ACT.Exp, bias=-1.2 * 0.3 + math.log(0.5), scale=-1.2)
+            if not square_on_vector:
+                nc.scalar.activation(bowls[h][:, d0:d1, :], bank[:], ACT.Square, bias=-ROOT * CENTRE, scale=ROOT)
+            for d in range(d0, d1):
+                nc.vector.scalar_tensor_tensor(half_logits[h][:, d, :], tails[h][:, d, :], shift[:, h, d : d + 1], bowls[h][:, d, :], ALU.add, ALU.subtract)
+
+        def back(h, d0, d1):
+            nc.scalar.activation(tanhs[h][:, d0:d1, :], half_logits[h][:, d0:d1, :], ACT.Tanh)
+            for d in range(d0, d1):
+                nxt = keep.tile([P, N], F32, name="running%d%d" % (h, d))
+                if d == 0:
+                    nc.vector.tensor_scalar(nxt[:], tanhs[h][:, d, :], first_slope[:, h : h + 1], first_level[:, h : h + 1], ALU.mult, ALU.add)
+                elif (h, d) == (HALVES - 1, D - 1):
+                    for b in range(N // P):
+                        cols = slice(b * P, (b + 1) * P)
+                        nc.vector.scalar_tensor_tensor(nxt[:, cols], tanhs[h][:, d, cols], root[:, h, d : d + 1], running[h][:, cols], ALU.subtract, ALU.mult)
                 else:
-                    nc.scalar.activation(th[:], half_logit[:], ACT.Tanh)
-                for e in range(2):
-                    d = 2 * pr + e
-                    nxt = keep.tile([P, N], F32, name="running%d%d" % (h, d))
-                    if d == 0:
-                        nc.vector.tensor_scalar(nxt[:], th[:, e, :], first_slope[:, h : h + 1], first_level[:, h : h + 1], ALU.mult, ALU.add)
-                    else:
-                        nc.vector.scalar_tensor_tensor(nxt[:], th[:, e, :], root[:, h, d : d + 1], running[:], ALU.subtract, ALU.mult)
-                    running = nxt
-            turned = psum.tile([P, N // P, P], F32, name="turned%d" % h)
-            for b in range(N // P):
-                nc.tensor.transpose(turned[:, b, :], running[:, b * P : (b + 1) * P], identity[:])
-            result = keep.tile([P, N // P, P], F32, name="result%d" % h)
-            nc.vector.tensor_scalar(result[:], turned[:], -1.0, 1.0, ALU.mult, ALU.add)
-            nc.sync.dma_start(out[:, h * P : (h + 1) * P].rearrange("(b p) v -> p b v", p=P), result[:])
+                    nc.vector.scalar_tensor_tensor(nxt[:], tanhs[h][:, d, :], root[:, h, d : d + 1], running[h][:], ALU.subtract, ALU.mult)
+                running[h] = nxt
+
+        front(0, 0, 1)
+        front(0, 1, 2)
+        front(0, 2, 4, True)
+        back(0, 0, 2)
+        front(1, 0, 2)
+        back(0, 2, 4)
+        front(1, 2, 3)
+        back(1, 0, 2)
+        front(1, 3, 4)
+        back(1, 2, 3)
+        back(1, 3, 4)
+
+        turned = psum.tile([P, N // P, P], F32, name="turned0", tag="y00")
+        for b in range(N // P):
+            nc.tensor.transpose(turned[:, b, :], running[0][:, b * P : (b + 1) * P], identity[:])
+        result = keep.tile([P, N // P, P], F32, name="result0")
+        nc.scalar.activation(result[:], turned[:], ACT.Copy, bias=1.0, scale=-1.0)
+        nc.sync.dma_start(out[:, 0:P].rearrange("(b p) v -> p b v", p=P), result[:])
+        for b in range(N // P):
+            last = psum.tile([P, P], F32, name="last%d" % b)
+            nc.tensor.transpose(last[:], running[1][:, b * P : (b + 1) * P], identity[:])
+            piece = keep.tile([P, P], F32, name="piece%d" % b)
+            if b == 0:
+                nc.scalar.activation(piece[:], last[:], ACT.Copy, bias=1.0, scale=-1.0)
+                nc.scalar.dma_start(out[b * P : (b + 1) * P, P : 2 * P], piece[:])
+            else:
+                nc.vector.tensor_scalar(piece[:], last[:], -1.0, 1.0, ALU.mult, ALU.add)
+                nc.sync.dma_start(out[b * P : (b + 1) * P, P : 2 * P], piece[:])

@@ -22,7 +22,7 @@ ACT = mybir.ActivationFunctionType
 
 CENTRE = (2 * 0.7 * 0.8 + 1.2) / (2 * 0.7)
 OFFSET = 0.7 * CENTRE * CENTRE - 0.7 * 0.8 * 0.8 + 1.2 * 0.3
-ROOT = math.sqrt(0.7 / 2)
+ROOT = math.sqrt(0.7)
 TINY = 1e-9
 LAG = 2
 
@@ -37,7 +37,7 @@ def tile_picked_yprot_prob_p_kernel(tc, x_words, x_scales, w1, prior, wgt, offs,
         nc.sync.dma_start(offsets[:], offs)
 
         weight = keep.tile([P, HALVES, D], F32, name="weight")
-        nc.gpsimd.dma_start(weight[:], wgt[0].rearrange("(h p d) -> p h d", h=HALVES, d=D))
+        nc.sync.dma_start(weight[:], wgt[0].rearrange("(h p d) -> p h d", h=HALVES, d=D))
         log_odds = keep.tile([P, HALVES, D], F32, name="log_odds")
         nc.gpsimd.dma_start(log_odds[:], prior[0].rearrange("(h p d) -> p h d", h=HALVES, d=D))
 
@@ -92,8 +92,6 @@ def tile_picked_yprot_prob_p_kernel(tc, x_words, x_scales, w1, prior, wgt, offs,
         nc.gpsimd.tensor_tensor(first_slope[:], later[:], slope[:, :, 0], ALU.mult)
         first_level = keep.tile([P, HALVES], F32, name="first_level")
         nc.gpsimd.tensor_tensor(first_level[:], first_slope[:], later[:], ALU.add)
-        shift = keep.tile([P, HALVES, D], F32, name="shift")
-        nc.scalar.activation(shift[:], log_odds[:], ACT.Copy, bias=0.5 * OFFSET, scale=0.5)
 
         codes = []
         for h in range(HALVES):
@@ -116,14 +114,14 @@ def tile_picked_yprot_prob_p_kernel(tc, x_words, x_scales, w1, prior, wgt, offs,
                 centred = keep.tile([P, d1 - d0, N], F32, name="centred%d%d" % (h, d0))
                 nc.vector.tensor_scalar(centred[:], bank[:], -CENTRE, ROOT, ALU.add, ALU.mult)
                 nc.vector.tensor_tensor(bowls[h][:, d0:d1, :], centred[:], centred[:], ALU.mult)
-            nc.scalar.activation(tails[h][:, d0:d1, :], bank[:], ACT.Exp, bias=-1.2 * 0.3 + math.log(0.5), scale=-1.2)
+            nc.scalar.activation(tails[h][:, d0:d1, :], bank[:], ACT.Exp, bias=-1.2 * 0.3, scale=-1.2)
             if not square_on_vector:
                 nc.scalar.activation(bowls[h][:, d0:d1, :], bank[:], ACT.Square, bias=-ROOT * CENTRE, scale=ROOT)
             for d in range(d0, d1):
-                nc.vector.scalar_tensor_tensor(half_logits[h][:, d, :], tails[h][:, d, :], shift[:, h, d : d + 1], bowls[h][:, d, :], ALU.add, ALU.subtract)
+                nc.vector.scalar_tensor_tensor(half_logits[h][:, d, :], tails[h][:, d, :], log_odds[:, h, d : d + 1], bowls[h][:, d, :], ALU.add, ALU.subtract)
 
         def back(h, d0, d1):
-            nc.scalar.activation(tanhs[h][:, d0:d1, :], half_logits[h][:, d0:d1, :], ACT.Tanh)
+            nc.scalar.activation(tanhs[h][:, d0:d1, :], half_logits[h][:, d0:d1, :], ACT.Tanh, bias=0.5 * OFFSET, scale=0.5)
             for d in range(d0, d1):
                 nxt = keep.tile([P, N], F32, name="running%d%d" % (h, d))
                 if d == 0:

@@ -23,7 +23,7 @@ ACT = mybir.ActivationFunctionType
 CENTRE = (2 * 0.7 * 0.8 + 1.2) / (2 * 0.7)
 OFFSET = 0.7 * CENTRE * CENTRE - 0.7 * 0.8 * 0.8 + 1.2 * 0.3
 ROOT = math.sqrt(0.7)
-TINY = 1e-9
+TINY = 1e-11
 LAG = 2
 
 
@@ -33,11 +33,11 @@ def tile_picked_yprot_prob_p_kernel(tc, x_words, x_scales, w1, prior, wgt, offs,
         keep = ctx.enter_context(tc.tile_pool(name="keep", bufs=1))
         psum = ctx.enter_context(tc.psum_pool(name="psum", bufs=1))
 
+        weight = keep.tile([P, HALVES, D], F32, name="weight")
+        nc.sync.dma_start(weight[:], wgt[0].rearrange("(h p d) -> p h d", h=HALVES, d=D))
         offsets = keep.tile([P, S // 16], U16, name="offsets")
         nc.sync.dma_start(offsets[:], offs)
 
-        weight = keep.tile([P, HALVES, D], F32, name="weight")
-        nc.sync.dma_start(weight[:], wgt[0].rearrange("(h p d) -> p h d", h=HALVES, d=D))
         log_odds = keep.tile([P, HALVES, D], F32, name="log_odds")
         nc.gpsimd.dma_start(log_odds[:], prior[0].rearrange("(h p d) -> p h d", h=HALVES, d=D))
 
@@ -58,13 +58,19 @@ def tile_picked_yprot_prob_p_kernel(tc, x_words, x_scales, w1, prior, wgt, offs,
         nc.vector.memset(zero[:], 0.0)
         nc.scalar.activation(warm[:], zero[:], ACT.Exp)
 
-        scale_dealt = []
+        picked_scales = []
         for h in range(HALVES):
             picked = keep.tile([P, D * P], U8, name="picked_scales%d" % h, align_bytes=64)
             nc.vector.tensor_copy(picked[:], scale_table[:].indirect(offsets[:, 32 * h : 32 * h + 32]))
-            dealt = keep.tile([P, D, P], U8, name="dealt_scales%d" % h, align_bytes=64)
-            nc.vector.tensor_copy(dealt[:], picked[:].rearrange("p (v d) -> p d v", d=D))
-            scale_dealt.append(dealt)
+            picked_scales.append(picked)
+        scale_dealt = {}
+
+        def deal_scales(h):
+            dealt = keep.tile([P, D, P], U8, name="dealt_scales%d" % h, tag="dealt_scales", align_bytes=64)
+            nc.vector.tensor_copy(dealt[:], picked_scales[h][:].rearrange("p (v d) -> p d v", d=D))
+            scale_dealt[h] = dealt
+
+        deal_scales(0)
 
         w_grouped = keep.tile([P, N, 4], BF16, name="w_grouped", tag="words0", align_bytes=64)
         nc.scalar.copy(w_grouped[:].rearrange("p (c i) j -> p c j i", i=4), w_raw[:].rearrange("p j (c i) -> p c j i", i=4))
@@ -72,26 +78,25 @@ def tile_picked_yprot_prob_p_kernel(tc, x_words, x_scales, w1, prior, wgt, offs,
         w_scales = keep.tile([P, N], U8, name="w_scales", align_bytes=64)
         nc.vector.quantize_mx(out=w_codes[:].bitcast(FP8X4), scales=w_scales[:], in_=w_grouped[:].rearrange("p m j -> p (m j)"))
 
-        squared = keep.tile([P, HALVES, D], F32, name="squared")
-        nc.gpsimd.tensor_tensor(squared[:], weight[:], weight[:], ALU.mult)
-        nudge = keep.tile([P, HALVES, D], F32, name="nudge")
-        nc.gpsimd.tensor_scalar(nudge[:], squared[:], TINY * TINY, 2 * TINY, ALU.is_lt, ALU.mult)
         safe = keep.tile([P, HALVES, D], F32, name="safe")
-        nc.gpsimd.tensor_tensor(safe[:], weight[:], nudge[:], ALU.add)
+        nc.vector.tensor_scalar_add(safe[:], weight[:], TINY)
         inverse = keep.tile([P, HALVES, D], F32, name="inverse")
         nc.vector.reciprocal(inverse[:], safe[:])
         root = keep.tile([P, HALVES, D], F32, name="root")
-        nc.gpsimd.tensor_scalar(root[:], inverse[:], 2.0, -1.0, ALU.mult, ALU.add)
+        nc.scalar.activation(root[:], inverse[:], ACT.Copy, bias=-1.0, scale=2.0)
         slope = keep.tile([P, HALVES, D], F32, name="slope")
-        nc.gpsimd.tensor_scalar(slope[:], safe[:], -0.5, 0.0, ALU.mult, ALU.add)
+        nc.scalar.activation(slope[:], weight[:], ACT.Copy, bias=-0.5 * TINY, scale=-0.5)
         pair = keep.tile([P, HALVES], F32, name="pair")
-        nc.gpsimd.tensor_tensor(pair[:], slope[:, :, 1], slope[:, :, 2], ALU.mult)
         later = keep.tile([P, HALVES], F32, name="later")
-        nc.gpsimd.tensor_tensor(later[:], pair[:], slope[:, :, 3], ALU.mult)
         first_slope = keep.tile([P, HALVES], F32, name="first_slope")
-        nc.gpsimd.tensor_tensor(first_slope[:], later[:], slope[:, :, 0], ALU.mult)
         first_level = keep.tile([P, HALVES], F32, name="first_level")
-        nc.gpsimd.tensor_tensor(first_level[:], first_slope[:], later[:], ALU.add)
+        for h in range(HALVES):
+            nc.scalar.activation(pair[:, h : h + 1], slope[:, h, 1:2], ACT.Copy, scale=slope[:, h, 2:3])
+        for h in range(HALVES):
+            nc.scalar.activation(later[:, h : h + 1], pair[:, h : h + 1], ACT.Copy, scale=slope[:, h, 3:4])
+        for h in range(HALVES):
+            nc.scalar.activation(first_slope[:, h : h + 1], slope[:, h, 0:1], ACT.Copy, scale=later[:, h : h + 1])
+            nc.scalar.activation(first_level[:, h : h + 1], slope[:, h, 0:1], ACT.Identity, scale=later[:, h : h + 1], bias=later[:, h : h + 1])
 
         codes = []
         for h in range(HALVES):
@@ -136,7 +141,8 @@ def tile_picked_yprot_prob_p_kernel(tc, x_words, x_scales, w1, prior, wgt, offs,
 
         front(0, 0, 1)
         front(0, 1, 2)
-        front(0, 2, 4, True)
+        front(0, 2, 4)
+        deal_scales(1)
         back(0, 0, 2)
         front(1, 0, 2)
         back(0, 2, 4)

@@ -6,7 +6,10 @@ from concourse.masks import make_identity
 
 K, T, S, D, N = 512, 2048, 1024, 4, 256
 P = 128
+PACK = 4
 HALVES = S // (D * P)
+LIST_COLUMNS = D * P // 16
+QUADRANT = 32
 FLOPS = 2 * K * S * N
 BYTES = K * T + (K // 32) * T + K * N * 4 + 2 * S * 4 + P * (S // 16) * 2 + N * (S // D) * 4
 
@@ -22,9 +25,8 @@ ACT = mybir.ActivationFunctionType
 
 CENTRE = (2 * 0.7 * 0.8 + 1.2) / (2 * 0.7)
 OFFSET = 0.7 * CENTRE * CENTRE - 0.7 * 0.8 * 0.8 + 1.2 * 0.3
-ROOT = math.sqrt(0.7)
+SQRT_CURVE = math.sqrt(0.7)
 TINY = 1e-11
-LAG = 2
 
 
 def tile_picked_yprot_prob_p_kernel(tc, x_words, x_scales, w1, prior, wgt, offs, out):
@@ -33,137 +35,152 @@ def tile_picked_yprot_prob_p_kernel(tc, x_words, x_scales, w1, prior, wgt, offs,
         keep = ctx.enter_context(tc.tile_pool(name="keep", bufs=1))
         psum = ctx.enter_context(tc.psum_pool(name="psum", bufs=1))
 
-        weight = keep.tile([P, HALVES, D], F32, name="weight")
-        nc.sync.dma_start(weight[:], wgt[0].rearrange("(h p d) -> p h d", h=HALVES, d=D))
         offsets = keep.tile([P, S // 16], U16, name="offsets")
         nc.sync.dma_start(offsets[:], offs)
 
-        log_odds = keep.tile([P, HALVES, D], F32, name="log_odds")
-        nc.gpsimd.dma_start(log_odds[:], prior[0].rearrange("(h p d) -> p h d", h=HALVES, d=D))
-
         scale_table = keep.tile([P, T], U8, name="scale_table", align_bytes=64)
-        for q in range(4):
-            nc.sync.dma_start(scale_table[32 * q : 32 * q + 32, :].bitcast(I32), x_scales[0, 4 * q : 4 * q + 4, :].bitcast(I32).partition_broadcast(8))
+        for q in range(P // QUADRANT):
+            nc.sync.dma_start(
+                scale_table[QUADRANT * q : QUADRANT * (q + 1), :].bitcast(I32),
+                x_scales[0, 4 * q : 4 * q + 4, :].bitcast(I32).partition_broadcast(QUADRANT // 4),
+            )
 
-        w_raw = keep.tile([P, 4, N], F32, name="w_raw")
-        nc.sync.dma_start(w_raw[:], w1.rearrange("(p j) m -> p j m", j=4))
+        w_raw = keep.tile([P, PACK, N], F32, name="w_raw")
+        nc.sync.dma_start(w_raw[:], w1.rearrange("(p j) m -> p j m", j=PACK))
         word_table = keep.tile([P, T], I32, name="word_table", align_bytes=64)
         nc.sync.dma_start(word_table[:], x_words[0].rearrange("p c r -> p (c r)").bitcast(I32))
+
+        log_odds = keep.tile([P, HALVES, D], F32, name="log_odds")
+        nc.sync.dma_start(log_odds[:], prior[0].rearrange("(h p d) -> p h d", h=HALVES, d=D))
+        weight = keep.tile([P, HALVES, D], F32, name="weight")
+        nc.sync.dma_start(weight[:], wgt[0].rearrange("(h p d) -> p h d", h=HALVES, d=D))
 
         identity = keep.tile([P, P], F32, name="identity")
         make_identity(nc, identity[:])
 
-        warm = keep.tile([P, 1], F32, name="warm")
+        one = keep.tile([P, 1], F32, name="one")
         zero = keep.tile([P, 1], F32, name="zero")
         nc.vector.memset(zero[:], 0.0)
-        nc.scalar.activation(warm[:], zero[:], ACT.Exp)
+        nc.scalar.activation(one[:], zero[:], ACT.Exp)
+
+        def entries(h):
+            return offsets[:, LIST_COLUMNS * h : LIST_COLUMNS * (h + 1)]
 
         picked_scales = []
         for h in range(HALVES):
             picked = keep.tile([P, D * P], U8, name="picked_scales%d" % h, align_bytes=64)
-            nc.vector.tensor_copy(picked[:], scale_table[:].indirect(offsets[:, 32 * h : 32 * h + 32]))
+            nc.vector.tensor_copy(picked[:], scale_table[:].indirect(entries(h)))
             picked_scales.append(picked)
-        scale_dealt = {}
+        x_scales_dealt = {}
 
         def deal_scales(h):
             dealt = keep.tile([P, D, P], U8, name="dealt_scales%d" % h, tag="dealt_scales", align_bytes=64)
             nc.vector.tensor_copy(dealt[:], picked_scales[h][:].rearrange("p (v d) -> p d v", d=D))
-            scale_dealt[h] = dealt
+            x_scales_dealt[h] = dealt
 
         deal_scales(0)
 
-        w_grouped = keep.tile([P, N, 4], BF16, name="w_grouped", tag="words0", align_bytes=64)
-        nc.scalar.copy(w_grouped[:].rearrange("p (c i) j -> p c j i", i=4), w_raw[:].rearrange("p j (c i) -> p c j i", i=4))
+        w_grouped = keep.tile([P, N, PACK], BF16, name="w_grouped", tag="words0", align_bytes=64)
+        nc.scalar.copy(
+            w_grouped[:].rearrange("p (c i) j -> p c j i", i=4),
+            w_raw[:].rearrange("p j (c i) -> p c j i", i=4),
+        )
         w_codes = keep.tile([P, N], U32, name="w_codes", align_bytes=64)
         w_scales = keep.tile([P, N], U8, name="w_scales", align_bytes=64)
         nc.vector.quantize_mx(out=w_codes[:].bitcast(FP8X4), scales=w_scales[:], in_=w_grouped[:].rearrange("p m j -> p (m j)"))
 
-        safe = keep.tile([P, HALVES, D], F32, name="safe")
-        nc.vector.tensor_scalar_add(safe[:], weight[:], TINY)
-        inverse = keep.tile([P, HALVES, D], F32, name="inverse")
-        nc.vector.reciprocal(inverse[:], safe[:])
-        root = keep.tile([P, HALVES, D], F32, name="root")
-        nc.scalar.activation(root[:], inverse[:], ACT.Copy, bias=-1.0, scale=2.0)
+        nudged = keep.tile([P, HALVES, D], F32, name="nudged")
+        nc.gpsimd.tensor_scalar(nudged[:], weight[:], 1.0, TINY, ALU.mult, ALU.add)
         slope = keep.tile([P, HALVES, D], F32, name="slope")
-        nc.scalar.activation(slope[:], weight[:], ACT.Copy, bias=-0.5 * TINY, scale=-0.5)
-        pair = keep.tile([P, HALVES], F32, name="pair")
-        later = keep.tile([P, HALVES], F32, name="later")
+        nc.gpsimd.tensor_scalar(slope[:], weight[:], -0.5, -0.5 * TINY, ALU.mult, ALU.add)
+        two_slopes = keep.tile([P, HALVES], F32, name="two_slopes")
+        nc.gpsimd.tensor_tensor(two_slopes[:], slope[:, :, 1], slope[:, :, 2], ALU.mult)
+        later_slopes = keep.tile([P, HALVES], F32, name="later_slopes")
+        nc.gpsimd.tensor_tensor(later_slopes[:], two_slopes[:], slope[:, :, 3], ALU.mult)
         first_slope = keep.tile([P, HALVES], F32, name="first_slope")
+        nc.gpsimd.tensor_tensor(first_slope[:], later_slopes[:], slope[:, :, 0], ALU.mult)
         first_level = keep.tile([P, HALVES], F32, name="first_level")
-        for h in range(HALVES):
-            nc.scalar.activation(pair[:, h : h + 1], slope[:, h, 1:2], ACT.Copy, scale=slope[:, h, 2:3])
-        for h in range(HALVES):
-            nc.scalar.activation(later[:, h : h + 1], pair[:, h : h + 1], ACT.Copy, scale=slope[:, h, 3:4])
-        for h in range(HALVES):
-            nc.scalar.activation(first_slope[:, h : h + 1], slope[:, h, 0:1], ACT.Copy, scale=later[:, h : h + 1])
-            nc.scalar.activation(first_level[:, h : h + 1], slope[:, h, 0:1], ACT.Identity, scale=later[:, h : h + 1], bias=later[:, h : h + 1])
+        nc.gpsimd.tensor_tensor(first_level[:], first_slope[:], later_slopes[:], ALU.add)
 
-        codes = []
+        x_codes = []
         for h in range(HALVES):
-            dealt_words = keep.tile([P, D, P], U32, name="picked_words%d" % h, tag="words%d" % h, align_bytes=64)
-            nc.vector.tensor_copy(dealt_words[:].rearrange("p d v -> p v d"), word_table[:].bitcast(U32).indirect(offsets[:, 32 * h : 32 * h + 32]))
-            codes.append(dealt_words)
+            words = keep.tile([P, D, P], U32, name="picked_words%d" % h, tag="words%d" % h, align_bytes=64)
+            nc.vector.tensor_copy(words[:].rearrange("p d v -> p v d"), word_table[:].bitcast(U32).indirect(entries(h)))
+            x_codes.append(words)
 
-        tails = [keep.tile([P, D, N], F32, name="tail%d" % h) for h in range(HALVES)]
-        bowls = [keep.tile([P, D, N], F32, name="bowl%d" % h) for h in range(HALVES)]
-        half_logits = [keep.tile([P, D, N], F32, name="half_logit%d" % h) for h in range(HALVES)]
-        tanhs = [keep.tile([P, D, N], F32, name="tanh%d" % h) for h in range(HALVES)]
-        running = {}
+        inverse = keep.tile([P, HALVES, D], F32, name="inverse")
+        nc.vector.reciprocal(inverse[:], nudged[:])
+        root = keep.tile([P, HALVES, D], F32, name="root")
+        nc.gpsimd.tensor_scalar(root[:], inverse[:], 2.0, -1.0, ALU.mult, ALU.add)
 
-        def front(h, d0, d1, square_on_vector=False):
+        exps = [keep.tile([P, D, N], F32, name="exps%d" % h) for h in range(HALVES)]
+        squares = [keep.tile([P, D, N], F32, name="squares%d" % h) for h in range(HALVES)]
+        logits = [keep.tile([P, D, N], F32, name="logits%d" % h) for h in range(HALVES)]
+        tanhs = [keep.tile([P, D, N], F32, name="tanhs%d" % h) for h in range(HALVES)]
+        product = {}
+
+        def score(h, d0, d1):
             bank = psum.tile([P, d1 - d0, N], F32, name="y%d%d" % (h, d0), tag="y%d%d" % (h, d0))
             for d in range(d0, d1):
-                nc.tensor.matmul_mx(out=bank[:, d - d0, :], lhsT=codes[h][:, d, :].bitcast(FP8X4), lhsT_scale=scale_dealt[h][:, d, :],
-                                    rhs=w_codes[:].bitcast(FP8X4), rhs_scale=w_scales[:], start=True, stop=True)
-            if square_on_vector:
-                centred = keep.tile([P, d1 - d0, N], F32, name="centred%d%d" % (h, d0))
-                nc.vector.tensor_scalar(centred[:], bank[:], -CENTRE, ROOT, ALU.add, ALU.mult)
-                nc.vector.tensor_tensor(bowls[h][:, d0:d1, :], centred[:], centred[:], ALU.mult)
-            nc.scalar.activation(tails[h][:, d0:d1, :], bank[:], ACT.Exp, bias=-1.2 * 0.3, scale=-1.2)
-            if not square_on_vector:
-                nc.scalar.activation(bowls[h][:, d0:d1, :], bank[:], ACT.Square, bias=-ROOT * CENTRE, scale=ROOT)
+                nc.tensor.matmul_mx(
+                    out=bank[:, d - d0, :],
+                    lhsT=x_codes[h][:, d, :].bitcast(FP8X4),
+                    lhsT_scale=x_scales_dealt[h][:, d, :],
+                    rhs=w_codes[:].bitcast(FP8X4),
+                    rhs_scale=w_scales[:],
+                    start=True,
+                    stop=True,
+                )
+            nc.scalar.activation(exps[h][:, d0:d1, :], bank[:], ACT.Exp, bias=-1.2 * 0.3, scale=-1.2)
+            nc.scalar.activation(squares[h][:, d0:d1, :], bank[:], ACT.Square, bias=-SQRT_CURVE * CENTRE, scale=SQRT_CURVE)
             for d in range(d0, d1):
-                nc.vector.scalar_tensor_tensor(half_logits[h][:, d, :], tails[h][:, d, :], log_odds[:, h, d : d + 1], bowls[h][:, d, :], ALU.add, ALU.subtract)
+                nc.vector.scalar_tensor_tensor(
+                    logits[h][:, d, :], exps[h][:, d, :], log_odds[:, h, d : d + 1], squares[h][:, d, :], ALU.add, ALU.subtract
+                )
 
-        def back(h, d0, d1):
-            nc.scalar.activation(tanhs[h][:, d0:d1, :], half_logits[h][:, d0:d1, :], ACT.Tanh, bias=0.5 * OFFSET, scale=0.5)
+        def multiply_in(h, d0, d1):
+            nc.scalar.activation(tanhs[h][:, d0:d1, :], logits[h][:, d0:d1, :], ACT.Tanh, bias=0.5 * OFFSET, scale=0.5)
             for d in range(d0, d1):
-                nxt = keep.tile([P, N], F32, name="running%d%d" % (h, d))
+                grown = keep.tile([P, N], F32, name="product%d%d" % (h, d))
                 if d == 0:
-                    nc.vector.tensor_scalar(nxt[:], tanhs[h][:, d, :], first_slope[:, h : h + 1], first_level[:, h : h + 1], ALU.mult, ALU.add)
-                elif (h, d) == (HALVES - 1, D - 1):
-                    for b in range(N // P):
-                        cols = slice(b * P, (b + 1) * P)
-                        nc.vector.scalar_tensor_tensor(nxt[:, cols], tanhs[h][:, d, cols], root[:, h, d : d + 1], running[h][:, cols], ALU.subtract, ALU.mult)
+                    nc.vector.tensor_scalar(
+                        grown[:], tanhs[h][:, d, :], first_slope[:, h : h + 1], first_level[:, h : h + 1], ALU.mult, ALU.add
+                    )
                 else:
-                    nc.vector.scalar_tensor_tensor(nxt[:], tanhs[h][:, d, :], root[:, h, d : d + 1], running[h][:], ALU.subtract, ALU.mult)
-                running[h] = nxt
+                    width = P if (h, d) == (HALVES - 1, D - 1) else N
+                    for m0 in range(0, N, width):
+                        cols = slice(m0, m0 + width)
+                        nc.vector.scalar_tensor_tensor(
+                            grown[:, cols], tanhs[h][:, d, cols], root[:, h, d : d + 1], product[h][:, cols], ALU.subtract, ALU.mult
+                        )
+                product[h] = grown
 
-        front(0, 0, 1)
-        front(0, 1, 2)
-        front(0, 2, 4)
+        score(0, 0, 1)
+        score(0, 1, 2)
+        score(0, 2, 4)
         deal_scales(1)
-        back(0, 0, 2)
-        front(1, 0, 2)
-        back(0, 2, 4)
-        front(1, 2, 3)
-        back(1, 0, 2)
-        front(1, 3, 4)
-        back(1, 2, 3)
-        back(1, 3, 4)
+        multiply_in(0, 0, 2)
+        score(1, 0, 2)
+        multiply_in(0, 2, 4)
+        score(1, 2, 3)
+        multiply_in(1, 0, 2)
+        score(1, 3, 4)
+        multiply_in(1, 2, 3)
+        multiply_in(1, 3, 4)
 
-        turned = psum.tile([P, N // P, P], F32, name="turned0", tag="y00")
+        turned = psum.tile([P, N // P, P], F32, name="turned", tag="y00")
         for b in range(N // P):
-            nc.tensor.transpose(turned[:, b, :], running[0][:, b * P : (b + 1) * P], identity[:])
-        result = keep.tile([P, N // P, P], F32, name="result0")
-        nc.scalar.activation(result[:], turned[:], ACT.Copy, bias=1.0, scale=-1.0)
+            nc.tensor.transpose(turned[:, b, :], product[0][:, b * P : (b + 1) * P], identity[:])
+        result = keep.tile([P, N // P, P], F32, name="result")
+        nc.scalar.activation(result[:], turned[:], ACT.Identity, bias=one[:], scale=-1.0)
         nc.sync.dma_start(out[:, 0:P].rearrange("(b p) v -> p b v", p=P), result[:])
+
         for b in range(N // P):
             last = psum.tile([P, P], F32, name="last%d" % b)
-            nc.tensor.transpose(last[:], running[1][:, b * P : (b + 1) * P], identity[:])
+            nc.tensor.transpose(last[:], product[1][:, b * P : (b + 1) * P], identity[:])
             piece = keep.tile([P, P], F32, name="piece%d" % b)
             if b == 0:
-                nc.scalar.activation(piece[:], last[:], ACT.Copy, bias=1.0, scale=-1.0)
+                nc.scalar.activation(piece[:], last[:], ACT.Identity, bias=one[:], scale=-1.0)
                 nc.scalar.dma_start(out[b * P : (b + 1) * P, P : 2 * P], piece[:])
             else:
                 nc.vector.tensor_scalar(piece[:], last[:], -1.0, 1.0, ALU.mult, ALU.add)

import math
from contextlib import ExitStack

import concourse.mybir as mybir
from concourse.masks import make_identity

K, T, S, D, N = 512, 2048, 1024, 4, 256
P = 128
PACK = 4
HALVES = S // (D * P)
LIST_COLUMNS = D * P // 16
QUADRANT = 32
FLOPS = 2 * K * S * N
BYTES = K * T + (K // 32) * T + K * N * 4 + 2 * S * 4 + P * (S // 16) * 2 + N * (S // D) * 4

F32 = mybir.dt.float32
BF16 = mybir.dt.bfloat16
I32 = mybir.dt.int32
U32 = mybir.dt.uint32
U16 = mybir.dt.uint16
U8 = mybir.dt.uint8
FP8X4 = mybir.dt.float8_e4m3fn_x4
ALU = mybir.AluOpType
ACT = mybir.ActivationFunctionType

CENTRE = (2 * 0.7 * 0.8 + 1.2) / (2 * 0.7)
OFFSET = 0.7 * CENTRE * CENTRE - 0.7 * 0.8 * 0.8 + 1.2 * 0.3
SQRT_CURVE = math.sqrt(0.7)
TINY = 1e-11


def tile_picked_yprot_prob_p_kernel(tc, x_words, x_scales, w1, prior, wgt, offs, out):
    nc = tc.nc
    with ExitStack() as ctx:
        keep = ctx.enter_context(tc.tile_pool(name="keep", bufs=1))
        psum = ctx.enter_context(tc.psum_pool(name="psum", bufs=1))

        offsets = keep.tile([P, S // 16], U16, name="offsets")
        nc.sync.dma_start(offsets[:], offs)

        scale_table = keep.tile([P, T], U8, name="scale_table", align_bytes=64)
        for q in range(P // QUADRANT):
            nc.sync.dma_start(
                scale_table[QUADRANT * q : QUADRANT * (q + 1), :].bitcast(I32),
                x_scales[0, 4 * q : 4 * q + 4, :].bitcast(I32).partition_broadcast(QUADRANT // 4),
            )

        w_raw = keep.tile([P, PACK, N], F32, name="w_raw")
        nc.sync.dma_start(w_raw[:], w1.rearrange("(p j) m -> p j m", j=PACK))
        word_table = keep.tile([P, T], I32, name="word_table", align_bytes=64)
        nc.sync.dma_start(word_table[:], x_words[0].rearrange("p c r -> p (c r)").bitcast(I32))

        log_odds = keep.tile([P, HALVES, D], F32, name="log_odds")
        nc.sync.dma_start(log_odds[:], prior[0].rearrange("(h p d) -> p h d", h=HALVES, d=D))
        weight = keep.tile([P, HALVES, D], F32, name="weight")
        nc.sync.dma_start(weight[:], wgt[0].rearrange("(h p d) -> p h d", h=HALVES, d=D))

        identity = keep.tile([P, P], F32, name="identity")
        make_identity(nc, identity[:])

        one = keep.tile([P, 1], F32, name="one")
        zero = keep.tile([P, 1], F32, name="zero")
        nc.vector.memset(zero[:], 0.0)
        nc.scalar.activation(one[:], zero[:], ACT.Exp)

        def entries(h):
            return offsets[:, LIST_COLUMNS * h : LIST_COLUMNS * (h + 1)]

        picked_scales = []
        for h in range(HALVES):
            picked = keep.tile([P, D * P], U8, name="picked_scales%d" % h, align_bytes=64)
            nc.vector.tensor_copy(picked[:], scale_table[:].indirect(entries(h)))
            picked_scales.append(picked)
        x_scales_dealt = {}

        def deal_scales(h):
            dealt = keep.tile([P, D, P], U8, name="dealt_scales%d" % h, tag="dealt_scales", align_bytes=64)
            nc.vector.tensor_copy(dealt[:], picked_scales[h][:].rearrange("p (v d) -> p d v", d=D))
            x_scales_dealt[h] = dealt

        deal_scales(0)

        w_grouped = keep.tile([P, N, PACK], BF16, name="w_grouped", tag="words0", align_bytes=64)
        nc.scalar.copy(
            w_grouped[:].rearrange("p (c i) j -> p c j i", i=4),
            w_raw[:].rearrange("p j (c i) -> p c j i", i=4),
        )
        w_codes = keep.tile([P, N], U32, name="w_codes", align_bytes=64)
        w_scales = keep.tile([P, N], U8, name="w_scales", align_bytes=64)
        nc.vector.quantize_mx(out=w_codes[:].bitcast(FP8X4), scales=w_scales[:], in_=w_grouped[:].rearrange("p m j -> p (m j)"))

        nudged = keep.tile([P, HALVES, D], F32, name="nudged")
        nc.gpsimd.tensor_scalar(nudged[:], weight[:], 1.0, TINY, ALU.mult, ALU.add)
        slope = keep.tile([P, HALVES, D], F32, name="slope")
        nc.gpsimd.tensor_scalar(slope[:], weight[:], -0.5, -0.5 * TINY, ALU.mult, ALU.add)
        two_slopes = keep.tile([P, HALVES], F32, name="two_slopes")
        nc.gpsimd.tensor_tensor(two_slopes[:], slope[:, :, 1], slope[:, :, 2], ALU.mult)
        later_slopes = keep.tile([P, HALVES], F32, name="later_slopes")
        nc.gpsimd.tensor_tensor(later_slopes[:], two_slopes[:], slope[:, :, 3], ALU.mult)
        first_slope = keep.tile([P, HALVES], F32, name="first_slope")
        nc.gpsimd.tensor_tensor(first_slope[:], later_slopes[:], slope[:, :, 0], ALU.mult)
        first_level = keep.tile([P, HALVES], F32, name="first_level")
        nc.gpsimd.tensor_tensor(first_level[:], first_slope[:], later_slopes[:], ALU.add)

        x_codes = []
        for h in range(HALVES):
            words = keep.tile([P, D, P], U32, name="picked_words%d" % h, tag="words%d" % h, align_bytes=64)
            nc.vector.tensor_copy(words[:].rearrange("p d v -> p v d"), word_table[:].bitcast(U32).indirect(entries(h)))
            x_codes.append(words)

        inverse = keep.tile([P, HALVES, D], F32, name="inverse")
        nc.vector.reciprocal(inverse[:], nudged[:])
        root = keep.tile([P, HALVES, D], F32, name="root")
        nc.gpsimd.tensor_scalar(root[:], inverse[:], 2.0, -1.0, ALU.mult, ALU.add)

        exps = [keep.tile([P, D, N], F32, name="exps%d" % h) for h in range(HALVES)]
        squares = [keep.tile([P, D, N], F32, name="squares%d" % h) for h in range(HALVES)]
        logits = [keep.tile([P, D, N], F32, name="logits%d" % h) for h in range(HALVES)]
        tanhs = [keep.tile([P, D, N], F32, name="tanhs%d" % h) for h in range(HALVES)]
        product = {}

        def score(h, d0, d1):
            bank = psum.tile([P, d1 - d0, N], F32, name="y%d%d" % (h, d0), tag="y%d%d" % (h, d0))
            for d in range(d0, d1):
                nc.tensor.matmul_mx(
                    out=bank[:, d - d0, :],
                    lhsT=x_codes[h][:, d, :].bitcast(FP8X4),
                    lhsT_scale=x_scales_dealt[h][:, d, :],
                    rhs=w_codes[:].bitcast(FP8X4),
                    rhs_scale=w_scales[:],
                    start=True,
                    stop=True,
                )
            nc.scalar.activation(exps[h][:, d0:d1, :], bank[:], ACT.Exp, bias=-1.2 * 0.3, scale=-1.2)
            nc.scalar.activation(squares[h][:, d0:d1, :], bank[:], ACT.Square, bias=-SQRT_CURVE * CENTRE, scale=SQRT_CURVE)
            for d in range(d0, d1):
                nc.vector.scalar_tensor_tensor(
                    logits[h][:, d, :], exps[h][:, d, :], log_odds[:, h, d : d + 1], squares[h][:, d, :], ALU.add, ALU.subtract
                )

        def multiply_in(h, d0, d1):
            nc.scalar.activation(tanhs[h][:, d0:d1, :], logits[h][:, d0:d1, :], ACT.Tanh, bias=0.5 * OFFSET, scale=0.5)
            for d in range(d0, d1):
                grown = keep.tile([P, N], F32, name="product%d%d" % (h, d))
                if d == 0:
                    nc.vector.tensor_scalar(
                        grown[:], tanhs[h][:, d, :], first_slope[:, h : h + 1], first_level[:, h : h + 1], ALU.mult, ALU.add
                    )
                else:
                    width = P if (h, d) == (HALVES - 1, D - 1) else N
                    for m0 in range(0, N, width):
                        cols = slice(m0, m0 + width)
                        nc.vector.scalar_tensor_tensor(
                            grown[:, cols], tanhs[h][:, d, cols], root[:, h, d : d + 1], product[h][:, cols], ALU.subtract, ALU.mult
                        )
                product[h] = grown

        score(0, 0, 1)
        score(0, 1, 2)
        score(0, 2, 4)
        deal_scales(1)
        multiply_in(0, 0, 2)
        score(1, 0, 2)
        multiply_in(0, 2, 4)
        score(1, 2, 3)
        multiply_in(1, 0, 2)
        score(1, 3, 4)
        multiply_in(1, 2, 3)
        multiply_in(1, 3, 4)

        turned = psum.tile([P, N // P, P], F32, name="turned", tag="y00")
        for b in range(N // P):
            nc.tensor.transpose(turned[:, b, :], product[0][:, b * P : (b + 1) * P], identity[:])
        result = keep.tile([P, N // P, P], F32, name="result")
        nc.scalar.activation(result[:], turned[:], ACT.Identity, bias=one[:], scale=-1.0)
        nc.sync.dma_start(out[:, 0:P].rearrange("(b p) v -> p b v", p=P), result[:])

        for b in range(N // P):
            last = psum.tile([P, P], F32, name="last%d" % b)
            nc.tensor.transpose(last[:], product[1][:, b * P : (b + 1) * P], identity[:])
            piece = keep.tile([P, P], F32, name="piece%d" % b)
            if b == 0:
                nc.scalar.activation(piece[:], last[:], ACT.Identity, bias=one[:], scale=-1.0)
                nc.scalar.dma_start(out[b * P : (b + 1) * P, P : 2 * P], piece[:])
            else:
                nc.vector.tensor_scalar(piece[:], last[:], -1.0, 1.0, ALU.mult, ALU.add)
                nc.sync.dma_start(out[b * P : (b + 1) * P, P : 2 * P], piece[:])
